import numpy as np
import ml_dtypes


def mxq(x, axis, fmt="e4m3"):
    dtype, down = {"e4m3": (ml_dtypes.float8_e4m3fn, 7), "e5m2": (ml_dtypes.float8_e5m2, 14)}[fmt]
    v = np.moveaxis(np.asarray(x, np.float32).astype(ml_dtypes.bfloat16).astype(np.float64), axis, -1)
    blocks = v.reshape(v.shape[:-1] + (-1, 32))
    amax = np.abs(blocks).max(-1, keepdims=True)
    byte = np.maximum(np.where(amax > 0, np.frexp(amax)[1] - 1 + 127, 0) - down, 1)
    scale = np.exp2(byte - 127.0)
    codes = (blocks / scale).astype(np.float32).astype(dtype).astype(np.float64)
    return np.moveaxis((codes * scale).reshape(v.shape), -1, axis)


WIDE = False


def mx_kscale(k):
    if not WIDE:
        return np.ones(k)
    levels = np.array([10, -10, 5, -5, 0])
    if k % 512:
        return np.exp2(np.random.permutation(np.resize(levels, k // 32))).repeat(32)
    a = np.empty((k // 512, 16))
    for p in range(k // 512):
        a[p, :8] = np.random.permutation(np.resize(levels, 8))
        for g in range(8):
            far = levels[np.abs(levels - a[p, g]) >= 10]
            a[p, g + 8] = far[np.random.randint(len(far))]
    return np.exp2(a.ravel()).repeat(32)


def f64(x):
    return np.asarray(x).astype(np.float64)


def striped(idx):
    return np.tile(idx.reshape(-1, 16).T, (8, 1)).astype(np.uint16)


def unstriped(offs):
    return offs[:16].T.reshape(-1).astype(np.int64)


def striped8(idx):
    return np.concatenate([x.reshape(-1, 16).T for x in idx]).astype(np.uint16)


def runs(offs, k):
    lists = np.stack([offs[16 * r : 16 * r + 16].T.reshape(-1) for r in range(8)]).astype(np.int64)
    return lists[np.arange(k) % 512 // 64]


def pack_weight(w):
    k, n = w.shape
    w = f64(np.asarray(w, np.float32).astype(ml_dtypes.bfloat16)).reshape(k // 32, 32, n)
    amax = np.abs(w).max(1)
    byte = np.clip(np.where(amax > 0, np.frexp(amax)[1] - 1 + 127 - 7, 1), 1, 254)
    scaled = (w * np.exp2(127.0 - byte)[:, None, :]).reshape(k, n).astype(np.float32)
    words = np.ascontiguousarray(scaled.reshape(k // 512, 128, 4, n).transpose(0, 1, 3, 2)).astype(ml_dtypes.float8_e4m3fn).view(np.uint8)
    return words, np.ascontiguousarray(byte.astype(np.uint8).reshape(k // 512, 16, n))


def unpack_weight(words, scales):
    g, p, n, _ = words.shape
    vals = np.ascontiguousarray(words).view(ml_dtypes.float8_e4m3fn).astype(np.float64) * np.repeat(np.exp2(scales.astype(np.float64) - 127.0), 8, axis=1)[..., None]
    return vals.transpose(0, 1, 3, 2).reshape(g * 512, n)

def planes(y):
    n, m = y.shape
    v = y.astype(np.float32).astype(ml_dtypes.bfloat16).astype(np.float64).reshape(n // 32, 32, m)
    top = np.abs(v).max(1)
    byte = np.clip(np.where(top > 0, np.frexp(top)[1] - 1 + 127 - 7, 1), 1, 254)
    codes = (v * np.exp2(127.0 - byte)[:, None, :]).reshape(n, m).astype(np.float32).astype(ml_dtypes.float8_e4m3fn).view(np.uint8)
    words = codes.reshape(n // 512, 128, 4, m).transpose(0, 1, 3, 2)
    return np.ascontiguousarray(words), np.ascontiguousarray(byte.astype(np.uint8).reshape(n // 512, 16, m))


K, T, S, V, H, J, W = 512, 2048, 512, 512, 512, 512, 256


def setup_inputs():
    n = np.random.standard_normal
    s = mx_kscale(K)[:, None]
    u = mx_kscale(S)
    packed_xT = pack_weight(n((K, T)) * s)
    packed_w1 = pack_weight(n((K, H)) / np.sqrt(K) / s)
    packed_w2 = pack_weight(n((K, H)) / np.sqrt(K) / s)
    packed_w3 = pack_weight(n((K, H)) / np.sqrt(K) / s)
    perm = np.stack([np.random.permutation(V) for _ in range(8)])
    return {
        "x_words": packed_xT[0],
        "x_scales": packed_xT[1],
        "w1_words": packed_w1[0],
        "w1_scales": packed_w1[1],
        "w2_words": packed_w2[0],
        "w2_scales": packed_w2[1],
        "w3_words": packed_w3[0],
        "w3_scales": packed_w3[1],
        "tab": np.random.uniform(0.4, 1.4, (H, J)).astype(np.float32),
        "ga": (np.random.uniform(0.5, 1.5, (H, 1)) * u[:, None]).astype(np.float32),
        "gb": (np.random.uniform(0.5, 1.5, (H, 1)) / u[:, None]).astype(np.float32),
        "offs": striped(np.random.permutation(T)[:S]),
        "two": striped(np.random.permutation(T)[:S]),
        "n1": striped8(np.stack([np.random.permutation(S) for _ in range(8)])),
        "n2": striped8(np.stack([np.random.permutation(S) for _ in range(8)])),
        "three": striped(np.random.permutation(T)[:V]),
        "n3": striped8(np.random.randint(0, J, (8, V))),
        "n4": striped8(np.stack([np.random.permutation(V) for _ in range(8)])),
        "n5": striped8(perm[:, :W]),
        "n6": striped8(perm[:, W:]),
    }


def reference(x_words, x_scales, w1_words, w1_scales, w2_words, w2_scales, w3_words, w3_scales, tab, ga, gb, offs, two, n1, n2, three, n3, n4, n5, n6):
    xq = unpack_weight(x_words, x_scales)[:, unstriped(offs)]
    y = unpack_weight(w1_words, w1_scales).T @ xq
    x_two = unpack_weight(x_words, x_scales)[:, unstriped(two)]
    d = unpack_weight(w2_words, w2_scales).T @ x_two
    z = f64(ga) * ((y - (y[np.arange(H)[:, None], runs(n1, H)])) / (np.abs(d) + np.abs(d[np.arange(H)[:, None], runs(n2, H)]) + 0.5))
    x_three = unpack_weight(x_words, x_scales)[:, unstriped(three)]
    b = unpack_weight(w3_words, w3_scales).T @ x_three
    z2 = f64(gb) * (b * (f64(tab)[np.arange(H)[:, None], runs(n3, H)]) - (0.5 * (b[np.arange(H)[:, None], runs(n4, H)])))
    s = 0.0625 * ((mxq(z, 0, "e4m3").T @ mxq(z2, 0, "e4m3")))
    pa = s[np.arange(S)[:, None], runs(n5, S)]
    pb = s[np.arange(S)[:, None], runs(n6, S)]
    rb = pa * pb
    ra = pa + pb
    ds = np.zeros((S, V))
    ds[np.arange(S)[:, None], runs(n5, S)] = ra
    out = ds.copy()
    out[np.arange(S)[:, None], runs(n6, S)] = rb
    return (out,) + planes(out)

@@ -1,0 +1,344 @@
+from contextlib import ExitStack
+
+import concourse.mybir as mybir
+from concourse.masks import make_identity
+
+FLOPS = 4 * 2 * 512 * 512 * 512
+
+F32 = mybir.dt.float32
+BF16 = mybir.dt.bfloat16
+I32 = mybir.dt.int32
+U32 = mybir.dt.uint32
+U16 = mybir.dt.uint16
+U8 = mybir.dt.uint8
+FP8X4 = mybir.dt.float8_e4m3fn_x4
+ACT = mybir.ActivationFunctionType
+ALU = mybir.AluOpType
+
+P = 128
+PACK = 4
+T = 2048
+N = 512
+HALF = 256
+
+
+def tile_picked_twknormbkindgbond_none_po_kernel(
+    tc, x_words, x_scales, w1_words, w1_scales, w2_words, w2_scales, w3_words, w3_scales,
+    tab, ga, gb, offs, two, n1, n2, three, n3, n4, n5, n6, out_0, out_1, out_2,
+):
+    nc = tc.nc
+    with ExitStack() as ctx:
+        keep = ctx.enter_context(tc.tile_pool(name="keep", bufs=1))
+        acc_pool = ctx.enter_context(tc.psum_pool(name="acc", bufs=4))
+        turn_pool = ctx.enter_context(tc.psum_pool(name="turn", bufs=4))
+
+        def sb(name, shape, dtype, tag=None):
+            return keep.tile(shape, dtype, name=name, tag=tag or name, align_bytes=64)
+
+        def load_list(name, src):
+            dst = keep.tile([P, src.shape[1]], U16, name=name)
+            nc.sync.dma_start(dst[:], src)
+            return dst
+
+        def load_words(name, src):
+            dst = sb(name, [P, src.shape[2]], U32)
+            nc.sync.dma_start(out=dst[:].bitcast(I32), in_=src[0].rearrange("p c r -> p (c r)").bitcast(I32))
+            return dst
+
+        def scale_tile(name, width):
+            dst = sb(name, [P, width], U8)
+            nc.gpsimd.memset(dst[:].bitcast(I32), 0)
+            return dst
+
+        def load_scales(dst, src, first=0, queue=nc.sync):
+            for q in range(4):
+                queue.dma_start(
+                    out=dst[32 * q + first : 32 * q + first + 4, :].bitcast(I32),
+                    in_=src[0, 4 * q : 4 * q + 4, :].bitcast(I32),
+                )
+
+        def load_gain(name, src):
+            dst = sb(name, [P, PACK], F32)
+            nc.sync.dma_start(out=dst[:], in_=src.rearrange("(p t) o -> p (t o)", t=PACK))
+            return dst
+
+        tab_rows = tab.rearrange("(p t) c -> p t c", t=PACK)
+
+        def load_tab(t):
+            dst = sb("tab%d" % t, [P, N], F32)
+            nc.sync.dma_start(out=dst[:], in_=tab_rows[:, t, :])
+            return dst
+
+        xs = scale_tile("xs", T)
+        w2s = scale_tile("w2s", N)
+        w13s = scale_tile("w13s", N)
+        load_scales(w13s, w3_scales, first=4, queue=nc.gpsimd)
+        ident = sb("ident", [P, P], F32)
+        make_identity(nc, ident[:])
+
+        load_scales(xs, x_scales)
+        l_two = load_list("l_two", two)
+        l_offs = load_list("l_offs", offs)
+        l_n3 = load_list("l_n3", n3)
+        tabs = [load_tab(0)]
+        l_three = load_list("l_three", three)
+        tabs.append(load_tab(1))
+        load_scales(w2s, w2_scales)
+        w2w = load_words("w2w", w2_words)
+        xw = load_words("xw", x_words)
+        tabs.append(load_tab(2))
+        w1w = load_words("w1w", w1_words)
+        load_scales(w13s, w1_scales)
+        w3w = load_words("w3w", w3_words)
+        tabs.append(load_tab(3))
+        l_n2 = load_list("l_n2", n2)
+        ga_sb = load_gain("ga_sb", ga)
+        gb_sb = load_gain("gb_sb", gb)
+        l_n1 = load_list("l_n1", n1)
+        l_n4 = load_list("l_n4", n4)
+        l_n5 = load_list("l_n5", n5)
+        l_n6 = load_list("l_n6", n6)
+
+        def pick_scales(name, lst):
+            dst = sb(name, [P, N], U8)
+            nc.vector.tensor_copy(dst[:], xs[:].indirect(lst[:]))
+            return dst
+
+        def pick_words(name, lst):
+            dst = sb(name, [P, N], U32)
+            nc.vector.tensor_copy(dst[:], xw[:].indirect(lst[:]))
+            return dst
+
+        def deal_words(name, src):
+            dst = sb(name, [P, N], U32)
+            nc.scalar.copy(
+                out=dst[:].rearrange("p (t c i) -> p c t i", t=PACK, i=4),
+                in_=src[:].rearrange("p (c i t) -> p c t i", t=PACK, i=4),
+            )
+            return dst
+
+        def deal_scales(name, src):
+            dst = sb(name, [P, N], U8)
+            nc.vector.tensor_copy(
+                out=dst[:].rearrange("p (t c i) -> p c t i", t=PACK, i=16),
+                in_=src[:].rearrange("p (c i t) -> p c t i", t=PACK, i=16),
+            )
+            return dst
+
+        def product(t, lhs_words, lhs_scales, rhs_words, rhs_scales, first=0, pool=acc_pool):
+            acc = pool.tile([P, rhs_words.shape[1]], F32, name="bank")
+            cols = slice(P * t, P * (t + 1))
+            nc.tensor.matmul_mx(
+                out=acc[:],
+                lhsT=lhs_words[:, cols].bitcast(FP8X4),
+                lhsT_scale=lhs_scales[first:P, cols],
+                rhs=rhs_words[:].bitcast(FP8X4),
+                rhs_scale=rhs_scales[:],
+                start=True,
+                stop=True,
+            )
+            return acc
+
+        def halves(lst):
+            return [(slice(HALF * k, HALF * (k + 1)), lst[:, 16 * k : 16 * (k + 1)]) for k in range(2)]
+
+        def fetch_scalar(name, window, lst):
+            dst = sb(name, [P, N], F32)
+            for cols, part in halves(lst):
+                nc.scalar.activation(out=dst[:, cols], in_=window[:].indirect(part), func=ACT.Copy)
+            return dst
+
+        two_s = pick_scales("two_s", l_two)
+        offs_s = pick_scales("offs_s", l_offs)
+        three_s = pick_scales("three_s", l_three)
+        tab_g = [fetch_scalar("tab_g0", tabs[0], l_n3)]
+        tab_g.append(fetch_scalar("tab_g1", tabs[1], l_n3))
+        w2d = deal_words("w2d", w2w)
+        w2sd = deal_scales("w2sd", w2s)
+        two_w = pick_words("two_w", l_two)
+        tab_g.append(fetch_scalar("tab_g2", tabs[2], l_n3))
+        w1d = deal_words("w1d", w1w)
+        offs_w = pick_words("offs_w", l_offs)
+        w13sd = deal_scales("w13sd", w13s)
+        three_w = pick_words("three_w", l_three)
+        w3d = deal_words("w3d", w3w)
+
+        d_abs = []
+        for t in range(PACK):
+            if t == 2:
+                tab_g.append(fetch_scalar("tab_g3", tabs[3], l_n3))
+            acc = product(t, w2d, w2sd, two_w, two_s)
+            dst = sb("d_abs%d" % t, [P, N], F32, tag={0: "tab2", 2: "tab3"}.get(t))
+            nc.scalar.activation(out=dst[:], in_=acc[:], func=ACT.Abs)
+            d_abs.append(dst)
+        y_sc = []
+        for t in range(PACK):
+            acc = product(t, w1d, w13sd, offs_w, offs_s)
+            dst = sb("y_sc%d" % t, [P, N], F32)
+            nc.scalar.activation(out=dst[:], in_=acc[:], func=ACT.Copy, scale=ga_sb[:, t : t + 1])
+            y_sc.append(dst)
+
+        def turn_and_add(first, second):
+            banks = [turn_pool.tile([P, 2, 2, P], F32, name="bank") for h in range(2)]
+            for e in range(2):
+                for h in range(2):
+                    for b in range(2):
+                        cols = slice(P * (2 * h + b), P * (2 * h + b + 1))
+                        nc.tensor.matmul(banks[h][:, b, e, :], first[e][:, cols], ident[:], start=True, stop=False, is_transpose=True)
+                        nc.tensor.matmul(banks[h][:, b, e, :], second[e][:, cols], ident[:], start=False, stop=True, is_transpose=True)
+            return banks
+
+        d_got = []
+        den = []
+        for t in range(PACK):
+            dst = sb("d_got%d" % t, [P, N], F32)
+            for cols, part in halves(l_n2):
+                nc.vector.tensor_copy(dst[:, cols], d_abs[t][:].indirect(part))
+            d_got.append(dst)
+            if t % 2 == 1:
+                den.append(turn_and_add(d_abs[t - 1 : t + 1], d_got[t - 1 : t + 1]))
+
+        b_acc = []
+        b_half = []
+        for t in range(PACK):
+            acc = product(t, w3d, w13sd, three_w, three_s, first=4)
+            dst = sb("b_half%d" % t, [P, N], F32)
+            nc.scalar.activation(out=dst[:], in_=acc[:], func=ACT.Copy, scale=-0.5)
+            b_acc.append(acc)
+            b_half.append(dst)
+
+        def inverse(u):
+            result = []
+            roots = []
+            for h in range(2):
+                root = sb("root%d%d" % (u, h), [P, N], F32)
+                nc.scalar.activation(
+                    out=root[:].rearrange("j (b p e) -> j b p e", b=2, e=2),
+                    in_=den[u][h][:].rearrange("j b e p -> j b p e"),
+                    func=ACT.Abs_reciprocal_sqrt,
+                    bias=0.5,
+                )
+                roots.append(root)
+            for h in range(2):
+                inv = sb("inv%d%d" % (u, h), [P, N], F32)
+                nc.scalar.activation(out=inv[:], in_=roots[h][:], func=ACT.Square)
+                result.append(inv)
+            return result
+
+        inv_den = [inverse(0)]
+        inv_den.append(inverse(1))
+
+        y_got = []
+        num = []
+        for t in range(PACK):
+            dst = sb("y_got%d" % t, [P, N], F32)
+            for cols, part in halves(l_n1):
+                nc.vector.tensor_scalar(dst[:, cols], y_sc[t][:].indirect(part), -1.0, 0.0, ALU.mult, ALU.add)
+            y_got.append(dst)
+            if t % 2 == 1:
+                num.append(turn_and_add(y_sc[t - 1 : t + 1], y_got[t - 1 : t + 1]))
+
+        b_tab = []
+        for t in range(PACK):
+            dst = sb("b_tab%d" % t, [P, N], F32)
+            nc.vector.scalar_tensor_tensor(dst[:], b_acc[t][:], gb_sb[:, t : t + 1], tab_g[t][:], ALU.mult, ALU.mult)
+            b_tab.append(dst)
+
+        back = [acc_pool.tile([P, 2, 2, P], F32, name="bank") for h in range(2)]
+        for u in range(2):
+            for h in range(2):
+                z_turned = sb("z_turned%d%d" % (u, h), [P, N], BF16)
+                nc.vector.tensor_tensor(
+                    z_turned[:].rearrange("j (b p e) -> j b p e", b=2, e=2),
+                    num[u][h][:].rearrange("j b e p -> j b p e"),
+                    inv_den[u][h][:].rearrange("j (b p e) -> j b p e", b=2, e=2),
+                    ALU.mult,
+                )
+                words = z_turned[:].bitcast(F32)
+                for b in range(2):
+                    nc.tensor.transpose(back[h][:, b, u, :], words[:, P * b : P * (b + 1)], ident[:])
+
+        z_grouped = sb("z_grouped", [P, PACK * N], BF16)
+        z_words = z_grouped[:].bitcast(F32).rearrange("p (t h b m u) -> p h t b m u", t=PACK, h=2, b=2, u=2)
+        z_codes = sb("z_codes", [P, N], U32)
+        z_scales = sb("z_scales", [P, N], U8)
+        s_rows = [sb("s%d" % t, [P, N], F32) for t in range(PACK)]
+        s_acc = []
+        for k, (cols, part) in enumerate(halves(l_n4)):
+            z2 = sb("z2_%d" % k, [P, PACK, HALF], F32)
+            for t in range(PACK):
+                tag = "z_turned%d%d" % (1 - t // 2, 1 - t % 2) if k == 1 else None
+                got = sb("b_got%d%d" % (k, t), [P, HALF], F32, tag=tag)
+                nc.scalar.activation(out=got[:], in_=b_half[t][:].indirect(part), func=ACT.Copy)
+                nc.vector.scalar_tensor_tensor(z2[:, t, :], got[:], gb_sb[:, t : t + 1], b_tab[t][:, cols], ALU.mult, ALU.add)
+            grouped = sb("z2_grouped%d" % k, [P, PACK * HALF], BF16)
+            nc.vector.tensor_copy(
+                out=grouped[:].rearrange("p (c i t) -> p c t i", t=PACK, i=4),
+                in_=z2[:].rearrange("p t (c i) -> p c t i", i=4),
+            )
+            if k == 0:
+                for h in range(2):
+                    nc.scalar.copy(out=z_words[:, h], in_=back[h][:].rearrange("p b u (m t) -> p t b m u", t=PACK))
+                nc.vector.quantize_mx(out=z_codes[:].bitcast(FP8X4), scales=z_scales[:], in_=z_grouped[:])
+            z2_codes = sb("z2_codes%d" % k, [P, HALF], U32)
+            z2_scales = sb("z2_scales%d" % k, [P, HALF], U8)
+            nc.vector.quantize_mx(out=z2_codes[:].bitcast(FP8X4), scales=z2_scales[:], in_=grouped[:])
+            s_acc.append([product(t, z_codes, z_scales, z2_codes, z2_scales, pool=(acc_pool, turn_pool)[k]) for t in range(PACK)])
+
+        def leave_bank(k, t):
+            nc.scalar.activation(out=s_rows[t][:, HALF * k : HALF * (k + 1)], in_=s_acc[k][t][:], func=ACT.Copy, scale=0.0625)
+
+        for t in range(PACK):
+            leave_bank(0, t)
+
+        out_rows = out_0.rearrange("(p t) c -> p t c", t=PACK)
+        out_grouped = [sb("out_grouped%d" % k, [P, HALF, PACK], BF16) for k in range(2)]
+        pairs = []
+        outs = []
+
+        def finish(t):
+            pa, pb = pairs[t]
+            nc.vector.tensor_tensor(outs[t][:].indirect(l_n6[:]), pa[:], pb[:], ALU.mult)
+            nc.sync.dma_start(out=out_rows[:, t, :], in_=outs[t][:])
+            for k in range(2):
+                src = outs[t][:, HALF * k : HALF * (k + 1)]
+                if k == 0 and t >= 2:
+                    nc.vector.tensor_copy(out=out_grouped[k][:, :, t], in_=src)
+                else:
+                    nc.scalar.copy(out=out_grouped[k][:, :, t], in_=src)
+
+        for t in range(PACK):
+            leave_bank(1, t)
+            s = s_rows[t]
+            pa = sb("pa%d" % t, [P, HALF], F32)
+            pb = sb("pb%d" % t, [P, HALF], F32)
+            nc.scalar.activation(out=pa[:], in_=s[:].indirect(l_n5[:]), func=ACT.Copy)
+            if t == 0:
+                nc.vector.tensor_copy(pb[:], s[:].indirect(l_n6[:]))
+            else:
+                nc.scalar.activation(out=pb[:], in_=s[:].indirect(l_n6[:]), func=ACT.Copy)
+            pairs.append((pa, pb))
+        for t in range(PACK):
+            pa, pb = pairs[t]
+            outs.append(sb("out%d" % t, [P, N], F32))
+            nc.vector.tensor_tensor(outs[t][:].indirect(l_n5[:]), pa[:], pb[:], ALU.add)
+            if t > 0:
+                finish(t - 1)
+        finish(PACK - 1)
+
+        out_scales = sb("out_scales", [P, N], U8)
+        words_hbm = out_1[0].rearrange("p c r -> p (c r)").bitcast(I32)
+        for k in range(2):
+            cols = slice(HALF * k, HALF * (k + 1))
+            codes = sb("out_codes%d" % k, [P, HALF], U32)
+            nc.vector.quantize_mx(
+                out=codes[:].bitcast(FP8X4),
+                scales=out_scales[:, cols],
+                in_=out_grouped[k][:].rearrange("p c t -> p (c t)"),
+            )
+            nc.sync.dma_start(out=words_hbm[:, cols], in_=codes[:].bitcast(I32))
+        for q in range(4):
+            nc.scalar.dma_start(
+                out=out_2[0, 4 * q : 4 * q + 4, :].bitcast(I32),
+                in_=out_scales[32 * q : 32 * q + 4, :].bitcast(I32),
+            )

@@ -69,6 +69,11 @@ def tile_picked_twknormbkindgbond_none_po_kernel(
             nc.sync.dma_start(out=dst[:], in_=tab_rows[:, t, :])
             return dst
 
+        warm_in = sb("warm_in", [P, 1], F32)
+        warm_out = sb("warm_out", [P, 1], F32)
+        nc.vector.memset(warm_in[:], 1.0)
+        nc.scalar.activation(out=warm_out[:], in_=warm_in[:], func=ACT.Abs_reciprocal_sqrt)
+
         xs = scale_tile("xs", T)
         w2s = scale_tile("w2s", N)
         w13s = scale_tile("w13s", N)

from contextlib import ExitStack

import concourse.mybir as mybir
from concourse.masks import make_identity

FLOPS = 4 * 2 * 512 * 512 * 512

F32 = mybir.dt.float32
BF16 = mybir.dt.bfloat16
I32 = mybir.dt.int32
U32 = mybir.dt.uint32
U16 = mybir.dt.uint16
U8 = mybir.dt.uint8
FP8X4 = mybir.dt.float8_e4m3fn_x4
ACT = mybir.ActivationFunctionType
ALU = mybir.AluOpType

P = 128
PACK = 4
T = 2048
N = 512
HALF = 256


def tile_picked_twknormbkindgbond_none_po_kernel(
    tc, x_words, x_scales, w1_words, w1_scales, w2_words, w2_scales, w3_words, w3_scales,
    tab, ga, gb, offs, two, n1, n2, three, n3, n4, n5, n6, out_0, out_1, out_2,
):
    nc = tc.nc
    with ExitStack() as ctx:
        keep = ctx.enter_context(tc.tile_pool(name="keep", bufs=1))
        acc_pool = ctx.enter_context(tc.psum_pool(name="acc", bufs=4))
        turn_pool = ctx.enter_context(tc.psum_pool(name="turn", bufs=4))

        def sb(name, shape, dtype, tag=None):
            return keep.tile(shape, dtype, name=name, tag=tag or name, align_bytes=64)

        def load_list(name, src):
            dst = keep.tile([P, src.shape[1]], U16, name=name)
            nc.sync.dma_start(dst[:], src)
            return dst

        def load_words(name, src):
            dst = sb(name, [P, src.shape[2]], U32)
            nc.sync.dma_start(out=dst[:].bitcast(I32), in_=src[0].rearrange("p c r -> p (c r)").bitcast(I32))
            return dst

        def scale_tile(name, width):
            dst = sb(name, [P, width], U8)
            nc.gpsimd.memset(dst[:].bitcast(I32), 0)
            return dst

        def load_scales(dst, src, first=0, queue=nc.sync):
            for q in range(4):
                queue.dma_start(
                    out=dst[32 * q + first : 32 * q + first + 4, :].bitcast(I32),
                    in_=src[0, 4 * q : 4 * q + 4, :].bitcast(I32),
                )

        def load_gain(name, src):
            dst = sb(name, [P, PACK], F32)
            nc.sync.dma_start(out=dst[:], in_=src.rearrange("(p t) o -> p (t o)", t=PACK))
            return dst

        tab_rows = tab.rearrange("(p t) c -> p t c", t=PACK)

        def load_tab(t):
            dst = sb("tab%d" % t, [P, N], F32)
            nc.sync.dma_start(out=dst[:], in_=tab_rows[:, t, :])
            return dst

        warm_in = sb("warm_in", [P, 1], F32)
        warm_out = sb("warm_out", [P, 1], F32)
        nc.vector.memset(warm_in[:], 1.0)
        nc.scalar.activation(out=warm_out[:], in_=warm_in[:], func=ACT.Abs_reciprocal_sqrt)

        xs = scale_tile("xs", T)
        w2s = scale_tile("w2s", N)
        w13s = scale_tile("w13s", N)
        load_scales(w13s, w3_scales, first=4, queue=nc.gpsimd)
        ident = sb("ident", [P, P], F32)
        make_identity(nc, ident[:])

        load_scales(xs, x_scales)
        l_two = load_list("l_two", two)
        l_offs = load_list("l_offs", offs)
        l_n3 = load_list("l_n3", n3)
        tabs = [load_tab(0)]
        l_three = load_list("l_three", three)
        tabs.append(load_tab(1))
        load_scales(w2s, w2_scales)
        w2w = load_words("w2w", w2_words)
        xw = load_words("xw", x_words)
        tabs.append(load_tab(2))
        w1w = load_words("w1w", w1_words)
        load_scales(w13s, w1_scales)
        w3w = load_words("w3w", w3_words)
        tabs.append(load_tab(3))
        l_n2 = load_list("l_n2", n2)
        ga_sb = load_gain("ga_sb", ga)
        gb_sb = load_gain("gb_sb", gb)
        l_n1 = load_list("l_n1", n1)
        l_n4 = load_list("l_n4", n4)
        l_n5 = load_list("l_n5", n5)
        l_n6 = load_list("l_n6", n6)

        def pick_scales(name, lst):
            dst = sb(name, [P, N], U8)
            nc.vector.tensor_copy(dst[:], xs[:].indirect(lst[:]))
            return dst

        def pick_words(name, lst):
            dst = sb(name, [P, N], U32)
            nc.vector.tensor_copy(dst[:], xw[:].indirect(lst[:]))
            return dst

        def deal_words(name, src):
            dst = sb(name, [P, N], U32)
            nc.scalar.copy(
                out=dst[:].rearrange("p (t c i) -> p c t i", t=PACK, i=4),
                in_=src[:].rearrange("p (c i t) -> p c t i", t=PACK, i=4),
            )
            return dst

        def deal_scales(name, src):
            dst = sb(name, [P, N], U8)
            nc.vector.tensor_copy(
                out=dst[:].rearrange("p (t c i) -> p c t i", t=PACK, i=16),
                in_=src[:].rearrange("p (c i t) -> p c t i", t=PACK, i=16),
            )
            return dst

        def product(t, lhs_words, lhs_scales, rhs_words, rhs_scales, first=0, pool=acc_pool):
            acc = pool.tile([P, rhs_words.shape[1]], F32, name="bank")
            cols = slice(P * t, P * (t + 1))
            nc.tensor.matmul_mx(
                out=acc[:],
                lhsT=lhs_words[:, cols].bitcast(FP8X4),
                lhsT_scale=lhs_scales[first:P, cols],
                rhs=rhs_words[:].bitcast(FP8X4),
                rhs_scale=rhs_scales[:],
                start=True,
                stop=True,
            )
            return acc

        def halves(lst):
            return [(slice(HALF * k, HALF * (k + 1)), lst[:, 16 * k : 16 * (k + 1)]) for k in range(2)]

        def fetch_scalar(name, window, lst):
            dst = sb(name, [P, N], F32)
            for cols, part in halves(lst):
                nc.scalar.activation(out=dst[:, cols], in_=window[:].indirect(part), func=ACT.Copy)
            return dst

        two_s = pick_scales("two_s", l_two)
        offs_s = pick_scales("offs_s", l_offs)
        three_s = pick_scales("three_s", l_three)
        tab_g = [fetch_scalar("tab_g0", tabs[0], l_n3)]
        tab_g.append(fetch_scalar("tab_g1", tabs[1], l_n3))
        w2d = deal_words("w2d", w2w)
        w2sd = deal_scales("w2sd", w2s)
        two_w = pick_words("two_w", l_two)
        tab_g.append(fetch_scalar("tab_g2", tabs[2], l_n3))
        w1d = deal_words("w1d", w1w)
        offs_w = pick_words("offs_w", l_offs)
        w13sd = deal_scales("w13sd", w13s)
        three_w = pick_words("three_w", l_three)
        w3d = deal_words("w3d", w3w)

        d_abs = []
        for t in range(PACK):
            if t == 2:
                tab_g.append(fetch_scalar("tab_g3", tabs[3], l_n3))
            acc = product(t, w2d, w2sd, two_w, two_s)
            dst = sb("d_abs%d" % t, [P, N], F32, tag={0: "tab2", 2: "tab3"}.get(t))
            nc.scalar.activation(out=dst[:], in_=acc[:], func=ACT.Abs)
            d_abs.append(dst)
        y_sc = []
        for t in range(PACK):
            acc = product(t, w1d, w13sd, offs_w, offs_s)
            dst = sb("y_sc%d" % t, [P, N], F32)
            nc.scalar.activation(out=dst[:], in_=acc[:], func=ACT.Copy, scale=ga_sb[:, t : t + 1])
            y_sc.append(dst)

        def turn_and_add(first, second):
            banks = [turn_pool.tile([P, 2, 2, P], F32, name="bank") for h in range(2)]
            for e in range(2):
                for h in range(2):
                    for b in range(2):
                        cols = slice(P * (2 * h + b), P * (2 * h + b + 1))
                        nc.tensor.matmul(banks[h][:, b, e, :], first[e][:, cols], ident[:], start=True, stop=False, is_transpose=True)
                        nc.tensor.matmul(banks[h][:, b, e, :], second[e][:, cols], ident[:], start=False, stop=True, is_transpose=True)
            return banks

        d_got = []
        den = []
        for t in range(PACK):
            dst = sb("d_got%d" % t, [P, N], F32)
            for cols, part in halves(l_n2):
                nc.vector.tensor_copy(dst[:, cols], d_abs[t][:].indirect(part))
            d_got.append(dst)
            if t % 2 == 1:
                den.append(turn_and_add(d_abs[t - 1 : t + 1], d_got[t - 1 : t + 1]))

        b_acc = []
        b_half = []
        for t in range(PACK):
            acc = product(t, w3d, w13sd, three_w, three_s, first=4)
            dst = sb("b_half%d" % t, [P, N], F32)
            nc.scalar.activation(out=dst[:], in_=acc[:], func=ACT.Copy, scale=-0.5)
            b_acc.append(acc)
            b_half.append(dst)

        def inverse(u):
            result = []
            roots = []
            for h in range(2):
                root = sb("root%d%d" % (u, h), [P, N], F32)
                nc.scalar.activation(
                    out=root[:].rearrange("j (b p e) -> j b p e", b=2, e=2),
                    in_=den[u][h][:].rearrange("j b e p -> j b p e"),
                    func=ACT.Abs_reciprocal_sqrt,
                    bias=0.5,
                )
                roots.append(root)
            for h in range(2):
                inv = sb("inv%d%d" % (u, h), [P, N], F32)
                nc.scalar.activation(out=inv[:], in_=roots[h][:], func=ACT.Square)
                result.append(inv)
            return result

        inv_den = [inverse(0)]
        inv_den.append(inverse(1))

        y_got = []
        num = []
        for t in range(PACK):
            dst = sb("y_got%d" % t, [P, N], F32)
            for cols, part in halves(l_n1):
                nc.vector.tensor_scalar(dst[:, cols], y_sc[t][:].indirect(part), -1.0, 0.0, ALU.mult, ALU.add)
            y_got.append(dst)
            if t % 2 == 1:
                num.append(turn_and_add(y_sc[t - 1 : t + 1], y_got[t - 1 : t + 1]))

        b_tab = []
        for t in range(PACK):
            dst = sb("b_tab%d" % t, [P, N], F32)
            nc.vector.scalar_tensor_tensor(dst[:], b_acc[t][:], gb_sb[:, t : t + 1], tab_g[t][:], ALU.mult, ALU.mult)
            b_tab.append(dst)

        back = [acc_pool.tile([P, 2, 2, P], F32, name="bank") for h in range(2)]
        for u in range(2):
            for h in range(2):
                z_turned = sb("z_turned%d%d" % (u, h), [P, N], BF16)
                nc.vector.tensor_tensor(
                    z_turned[:].rearrange("j (b p e) -> j b p e", b=2, e=2),
                    num[u][h][:].rearrange("j b e p -> j b p e"),
                    inv_den[u][h][:].rearrange("j (b p e) -> j b p e", b=2, e=2),
                    ALU.mult,
                )
                words = z_turned[:].bitcast(F32)
                for b in range(2):
                    nc.tensor.transpose(back[h][:, b, u, :], words[:, P * b : P * (b + 1)], ident[:])

        z_grouped = sb("z_grouped", [P, PACK * N], BF16)
        z_words = z_grouped[:].bitcast(F32).rearrange("p (t h b m u) -> p h t b m u", t=PACK, h=2, b=2, u=2)
        z_codes = sb("z_codes", [P, N], U32)
        z_scales = sb("z_scales", [P, N], U8)
        s_rows = [sb("s%d" % t, [P, N], F32) for t in range(PACK)]
        s_acc = []
        for k, (cols, part) in enumerate(halves(l_n4)):
            z2 = sb("z2_%d" % k, [P, PACK, HALF], F32)
            for t in range(PACK):
                tag = "z_turned%d%d" % (1 - t // 2, 1 - t % 2) if k == 1 else None
                got = sb("b_got%d%d" % (k, t), [P, HALF], F32, tag=tag)
                nc.scalar.activation(out=got[:], in_=b_half[t][:].indirect(part), func=ACT.Copy)
                nc.vector.scalar_tensor_tensor(z2[:, t, :], got[:], gb_sb[:, t : t + 1], b_tab[t][:, cols], ALU.mult, ALU.add)
            grouped = sb("z2_grouped%d" % k, [P, PACK * HALF], BF16)
            nc.vector.tensor_copy(
                out=grouped[:].rearrange("p (c i t) -> p c t i", t=PACK, i=4),
                in_=z2[:].rearrange("p t (c i) -> p c t i", i=4),
            )
            if k == 0:
                for h in range(2):
                    nc.scalar.copy(out=z_words[:, h], in_=back[h][:].rearrange("p b u (m t) -> p t b m u", t=PACK))
                nc.vector.quantize_mx(out=z_codes[:].bitcast(FP8X4), scales=z_scales[:], in_=z_grouped[:])
            z2_codes = sb("z2_codes%d" % k, [P, HALF], U32)
            z2_scales = sb("z2_scales%d" % k, [P, HALF], U8)
            nc.vector.quantize_mx(out=z2_codes[:].bitcast(FP8X4), scales=z2_scales[:], in_=grouped[:])
            s_acc.append([product(t, z_codes, z_scales, z2_codes, z2_scales, pool=(acc_pool, turn_pool)[k]) for t in range(PACK)])

        def leave_bank(k, t):
            nc.scalar.activation(out=s_rows[t][:, HALF * k : HALF * (k + 1)], in_=s_acc[k][t][:], func=ACT.Copy, scale=0.0625)

        for t in range(PACK):
            leave_bank(0, t)

        out_rows = out_0.rearrange("(p t) c -> p t c", t=PACK)
        out_grouped = [sb("out_grouped%d" % k, [P, HALF, PACK], BF16) for k in range(2)]
        pairs = []
        outs = []

        def finish(t):
            pa, pb = pairs[t]
            nc.vector.tensor_tensor(outs[t][:].indirect(l_n6[:]), pa[:], pb[:], ALU.mult)
            nc.sync.dma_start(out=out_rows[:, t, :], in_=outs[t][:])
            for k in range(2):
                src = outs[t][:, HALF * k : HALF * (k + 1)]
                if k == 0 and t >= 2:
                    nc.vector.tensor_copy(out=out_grouped[k][:, :, t], in_=src)
                else:
                    nc.scalar.copy(out=out_grouped[k][:, :, t], in_=src)

        for t in range(PACK):
            leave_bank(1, t)
            s = s_rows[t]
            pa = sb("pa%d" % t, [P, HALF], F32)
            pb = sb("pb%d" % t, [P, HALF], F32)
            nc.scalar.activation(out=pa[:], in_=s[:].indirect(l_n5[:]), func=ACT.Copy)
            if t == 0:
                nc.vector.tensor_copy(pb[:], s[:].indirect(l_n6[:]))
            else:
                nc.scalar.activation(out=pb[:], in_=s[:].indirect(l_n6[:]), func=ACT.Copy)
            pairs.append((pa, pb))
        for t in range(PACK):
            pa, pb = pairs[t]
            outs.append(sb("out%d" % t, [P, N], F32))
            nc.vector.tensor_tensor(outs[t][:].indirect(l_n5[:]), pa[:], pb[:], ALU.add)
            if t > 0:
                finish(t - 1)
        finish(PACK - 1)

        out_scales = sb("out_scales", [P, N], U8)
        words_hbm = out_1[0].rearrange("p c r -> p (c r)").bitcast(I32)
        for k in range(2):
            cols = slice(HALF * k, HALF * (k + 1))
            codes = sb("out_codes%d" % k, [P, HALF], U32)
            nc.vector.quantize_mx(
                out=codes[:].bitcast(FP8X4),
                scales=out_scales[:, cols],
                in_=out_grouped[k][:].rearrange("p c t -> p (c t)"),
            )
            nc.sync.dma_start(out=words_hbm[:, cols], in_=codes[:].bitcast(I32))
        for q in range(4):
            nc.scalar.dma_start(
                out=out_2[0, 4 * q : 4 * q + 4, :].bitcast(I32),
                in_=out_scales[32 * q : 32 * q + 4, :].bitcast(I32),
            )
